import numpy as np
import ml_dtypes


def mxq(x, axis, fmt="e4m3"):
    dtype, down = {"e4m3": (ml_dtypes.float8_e4m3fn, 7), "e5m2": (ml_dtypes.float8_e5m2, 14)}[fmt]
    v = np.moveaxis(np.asarray(x, np.float32).astype(ml_dtypes.bfloat16).astype(np.float64), axis, -1)
    blocks = v.reshape(v.shape[:-1] + (-1, 32))
    amax = np.abs(blocks).max(-1, keepdims=True)
    byte = np.maximum(np.where(amax > 0, np.frexp(amax)[1] - 1 + 127, 0) - down, 1)
    scale = np.exp2(byte - 127.0)
    codes = (blocks / scale).astype(np.float32).astype(dtype).astype(np.float64)
    return np.moveaxis((codes * scale).reshape(v.shape), -1, axis)


WIDE = False


def mx_kscale(k):
    if not WIDE:
        return np.ones(k)
    levels = np.array([10, -10, 5, -5, 0])
    if k % 512:
        return np.exp2(np.random.permutation(np.resize(levels, k // 32))).repeat(32)
    a = np.empty((k // 512, 16))
    for p in range(k // 512):
        a[p, :8] = np.random.permutation(np.resize(levels, 8))
        for g in range(8):
            far = levels[np.abs(levels - a[p, g]) >= 10]
            a[p, g + 8] = far[np.random.randint(len(far))]
    return np.exp2(a.ravel()).repeat(32)


def f64(x):
    return np.asarray(x).astype(np.float64)


def striped(idx):
    return np.tile(idx.reshape(-1, 16).T, (8, 1)).astype(np.uint16)


def unstriped(offs):
    return offs[:16].T.reshape(-1).astype(np.int64)


E2M1 = np.array([0.0, 0.5, 1.0, 1.5, 2.0, 3.0, 4.0, 6.0, -0.0, -0.5, -1.0, -1.5, -2.0, -3.0, -4.0, -6.0])


def pack_weight(w, fmt):
    k, n = w.shape
    w = f64(np.asarray(w, np.float32).astype(ml_dtypes.bfloat16)).reshape(k // 32, 32, n)
    amax = np.abs(w).max(1)
    if fmt == "e4m3":
        byte = np.frexp(amax)[1] - 1 + 127 - 7
    else:
        mant, ex = np.frexp(amax / 6.0)
        byte = np.where(mant > 0.5, ex, ex - 1) + 127
    byte = np.clip(np.where(amax > 0, byte, 1), 1, 254)
    scaled = (w * np.exp2(127.0 - byte)[:, None, :]).reshape(k, n).astype(np.float32)
    by_word = np.ascontiguousarray(scaled.reshape(k // 512, 128, 4, n).transpose(0, 1, 3, 2))
    if fmt == "e4m3":
        words = by_word.astype(ml_dtypes.float8_e4m3fn).view(np.uint8)
    else:
        c = by_word.astype(ml_dtypes.float4_e2m1fn).view(np.uint8) & 0xF
        words = (c[..., 0::2] | (c[..., 1::2] << 4)).reshape(k // 512, 128, 2 * n)
    return np.ascontiguousarray(words), np.ascontiguousarray(byte.astype(np.uint8).reshape(k // 512, 16, n))


def unpack_weight(words, scales, fmt):
    g, _, n = scales.shape
    words = np.ascontiguousarray(words).reshape(g, 128, n, -1)
    if fmt == "e4m3":
        vals = words.view(ml_dtypes.float8_e4m3fn).astype(np.float64)
    else:
        nib = np.empty((g, 128, n, 4), np.uint8)
        nib[..., 0::2] = words & 0xF
        nib[..., 1::2] = words >> 4
        vals = E2M1[nib]
    vals = vals * np.repeat(np.exp2(scales.astype(np.float64) - 127.0), 8, axis=1)[..., None]
    return vals.transpose(0, 1, 3, 2).reshape(g * 512, n)


def gelu(v):
    return 0.5 * v * (1.0 + np.tanh(np.sqrt(2.0 / np.pi) * (v + 0.044715 * v**3)))


K, T, S, S2 = 1024, 2048, 1024, 512

def setup_inputs():
    n = np.random.standard_normal
    s = mx_kscale(K)[:, None]
    d = {}
    d["tab_words"], d["tab_scales"] = pack_weight(n((K, T)) * s, "e4m3")
    d["offs"] = striped(np.random.permutation(T)[:S])
    d["offs2"] = striped(np.random.permutation(T)[:S2])
    d["w1"] = (1.5 * n((K, K)) / K / s / s.T).astype(np.float32)
    d["w4_words"], d["w4_scales"] = pack_weight(1.5 * n((K, S2)) / K ** 0.5 / s, "e2m1")
    d["b4"] = (0.5 * n(S2)).astype(np.float32)
    return d

def reference(tab_words, tab_scales, offs, offs2, w1, w4_words, w4_scales, b4):
    TW = unpack_weight(tab_words, tab_scales, "e4m3")
    v = TW[:, unstriped(offs)]
    v2 = TW[:, unstriped(offs2)]
    w4 = unpack_weight(w4_words, w4_scales, "e2m1")
    h = np.abs(mxq(f64(w1), 0, "e4m3").T @ v)
    e = v2.T @ mxq(h, 0, "e4m3")
    skip = (w4.T @ v) + f64(b4)[:, None]
    return e * np.tanh(skip) + skip

@@ -1,0 +1,264 @@
+from contextlib import ExitStack
+
+import concourse.mybir as mybir
+
+K, T, S, S2 = 1024, 2048, 1024, 512
+FLOPS = 2 * K * K * S + 2 * K * S2 * S + 2 * K * S2 * S
+
+F32 = mybir.dt.float32
+BF16 = mybir.dt.bfloat16
+I32 = mybir.dt.int32
+U32 = mybir.dt.uint32
+U16 = mybir.dt.uint16
+U8 = mybir.dt.uint8
+FP8X4 = mybir.dt.float8_e4m3fn_x4
+FP4X4 = mybir.dt.float4_e2m1fn_x4
+ACT = mybir.ActivationFunctionType
+ALU = mybir.AluOpType
+
+P = 128
+PACK = 4
+KP = P * PACK
+PASSES = K // KP
+HALF = 512
+QUART = 256
+NQ = S // QUART
+HN = 128
+
+
+def tile_list_exam_clash_estimator_kernel(tc, tab_words, tab_scales, offs, offs2, w1, w4_words, w4_scales, b4, out):
+    nc = tc.nc
+    with ExitStack() as ctx:
+        keep = ctx.enter_context(tc.tile_pool(name="keep", bufs=1))
+        ring = ctx.enter_context(tc.tile_pool(name="ring", bufs=3))
+        psum = ctx.enter_context(tc.psum_pool(name="psum", bufs=2))
+
+        idx = keep.tile([P, S // 16], U16, name="idx")
+        idx2 = keep.tile([P, S2 // 16], U16, name="idx2")
+        tab_s = keep.tile([P, T], U8, name="tab_s", tag="tab_s", align_bytes=64)
+        tab_w = [keep.tile([P, T], I32, name="tab_w%d" % a, align_bytes=64) for a in range(PASSES)]
+        w4_w = keep.tile([P, PASSES, 2 * S2], U8, name="w4_w", align_bytes=64)
+        w4_s = keep.tile([P, PASSES, S2], U8, name="w4_s", align_bytes=64)
+        v_s1 = keep.tile([P, S], U8, name="v_s1", align_bytes=64)
+        bias = keep.tile([P, S2 // P], F32, name="bias")
+
+        def load_w1(a, b, c0, width, tag):
+            raw = keep.tile([P, PACK, width], F32, name="raw%d%d_%d" % (a, b, c0), tag=tag, align_bytes=64)
+            nc.sync.dma_start(
+                out=raw[:],
+                in_=w1[KP * a : KP * (a + 1), KP * b + c0 : KP * b + c0 + width].rearrange("(p j) c -> p j c", j=PACK),
+            )
+            return raw
+
+        def load_tab(a):
+            nc.sync.dma_start(out=tab_w[a][:], in_=tab_words[a].rearrange("p t i -> p (t i)").bitcast(I32))
+
+        def cast_w1(engine, grouped, raw, c0, m0, m1):
+            dst = grouped[:, :, m0:m1, :].rearrange("p t m j -> p m j t")
+            src = raw[:, :, PACK * m0 - c0 : PACK * m1 - c0].rearrange("p j (m t) -> p m j t", t=PACK)
+            if engine == "scalar":
+                nc.scalar.copy(out=dst, in_=src)
+            elif engine == "gpsimd":
+                nc.gpsimd.tensor_scalar(out=dst, in0=src, scalar1=1.0, scalar2=0.0, op0=ALU.mult, op1=ALU.add)
+            else:
+                nc.vector.tensor_copy(out=dst, in_=src)
+
+        w1_w = {}
+        w1_s = {}
+
+        def quantize_w1(a, b, grouped, parts):
+            w1_w[a, b] = keep.tile([P, KP], U32, name="w1_w%d%d" % (a, b), align_bytes=64)
+            w1_s[a, b] = keep.tile([P, KP], U8, name="w1_s%d%d" % (a, b), align_bytes=64)
+            nt = PACK // parts
+            for part in range(parts):
+                cols = slice(P * nt * part, P * nt * (part + 1))
+                nc.vector.quantize_mx(
+                    out=w1_w[a, b][:, cols].bitcast(FP8X4),
+                    scales=w1_s[a, b][:, cols],
+                    in_=grouped[:, nt * part : nt * (part + 1), :, :].rearrange("p t m j -> p (t m j)"),
+                )
+
+        def grouped_tile(a, b):
+            return keep.tile([P, PACK, P, PACK], BF16, name="grouped%d%d" % (a, b), tag="g%d%d" % (a, b), align_bytes=64)
+
+        def load_tab_scales():
+            for quad in range(4):
+                nc.sync.dma_start(
+                    out=tab_s[32 * quad : 32 * quad + 8, :].bitcast(I32),
+                    in_=tab_scales[:, 4 * quad : 4 * quad + 4, :].bitcast(I32),
+                )
+
+        def load_w4_words():
+            nc.sync.dma_start(out=w4_w[:].bitcast(I32), in_=w4_words.rearrange("a p n -> p a n").bitcast(I32))
+
+        def load_w4_scales():
+            for quad in range(4):
+                nc.sync.dma_start(
+                    out=w4_s[32 * quad : 32 * quad + 4, :, :].bitcast(I32),
+                    in_=w4_scales[:, 4 * quad : 4 * quad + 4, :].rearrange("a r n -> r a n").bitcast(I32),
+                )
+
+        def load_bias():
+            with nc.allow_non_contiguous_dma(reason="one bias value a partition"):
+                nc.sync.dma_start(out=bias[:], in_=b4.rearrange("(c p) -> p c", p=P))
+
+        nc.gpsimd.memset(tab_s[:].bitcast(I32), 0)
+        nc.gpsimd.memset(w4_s[:].bitcast(I32), 0)
+        nc.gpsimd.memset(v_s1[:].bitcast(I32), 0)
+        nc.sync.dma_start(idx[:], offs)
+        nc.sync.dma_start(idx2[:], offs2)
+        load_w4_words()
+        load_tab_scales()
+        load_tab(0)
+        raw00 = load_w1(0, 0, 0, KP, "raw00")
+        load_w4_scales()
+        load_bias()
+        raw10 = load_w1(1, 0, 0, KP, "raw10")
+        load_tab(1)
+        raw01 = load_w1(0, 1, 0, KP, "raw00")
+        raw11 = load_w1(1, 1, 0, KP, "raw10")
+
+        v_s = keep.tile([P, S], U8, name="v_s", align_bytes=64)
+        v2_s = keep.tile([P, S2], U8, name="v2_s", align_bytes=64)
+
+        def gather_scales():
+            nc.vector.tensor_copy(v_s[:], tab_s[:].indirect(idx[:]))
+            nc.gpsimd.dma_start(out=v_s1[0:100, :].bitcast(I32), in_=v_s[4:104, :].bitcast(I32))
+
+        def gather_scales2():
+            nc.vector.tensor_copy(v2_s[:], tab_s[:].indirect(idx2[:]))
+
+        v_w = {}
+        v2_w = {}
+
+        def gather_v(a, q0, nq, tag):
+            picked = keep.tile([P, nq * QUART], U32, name="v_w%d%d" % (a, q0), tag=tag, align_bytes=64)
+            cols = slice(q0 * QUART // 16, (q0 + nq) * QUART // 16)
+            nc.vector.tensor_copy(picked[:], tab_w[a][:].bitcast(U32).indirect(idx[:, cols]))
+            for q in range(nq):
+                v_w[a, q0 + q] = picked[:, QUART * q : QUART * (q + 1)]
+
+        def gather_v2(a, tag):
+            v2_w[a] = keep.tile([P, S2], U32, name="v2_w%d" % a, tag=tag, align_bytes=64)
+            nc.vector.tensor_copy(v2_w[a][:], tab_w[a][:].bitcast(U32).indirect(idx2[:]))
+
+        def v_words(a, j0, n):
+            return v_w[a, j0 // QUART][:, j0 % QUART : j0 % QUART + n].bitcast(FP8X4)
+
+        skip_bank = {}
+        bend = {}
+
+        def skip_stage(q):
+            j0 = QUART * q
+            for mp in range(2):
+                bank = psum.tile([P, 2, QUART], F32, name="skip_bank", tag="skip", bufs=3)
+                for a in range(PASSES):
+                    for mi in range(2):
+                        m = 2 * mp + mi
+                        plane = v_s if a == 0 else v_s1
+                        nc.tensor.matmul_mx(
+                            out=bank[:, mi, :],
+                            lhsT=w4_w[:, a, 2 * P * m : 2 * P * (m + 1)].bitcast(FP4X4),
+                            lhsT_scale=w4_s[:, a, P * m : P * (m + 1)],
+                            rhs=v_words(a, j0, QUART),
+                            rhs_scale=plane[:, j0 : j0 + QUART],
+                            start=(a == 0 and mi == 0),
+                            stop=(a == PASSES - 1 and mi == 1),
+                        )
+                skip_bank[q, mp] = bank
+
+        def tanh_stage(q):
+            for mp in range(2):
+                bend[q, mp] = keep.tile([P, 2, QUART], F32, name="bend%d%d" % (q, mp))
+                for mi in range(2):
+                    m = 2 * mp + mi
+                    nc.scalar.activation(out=bend[q, mp][:, mi, :], in_=skip_bank[q, mp][:, mi, :], func=ACT.Tanh, bias=bias[:, m : m + 1])
+
+        h_w = {}
+        h_s = {}
+
+        def h_stage(b, q):
+            hb = ring.tile([P, QUART, PACK], BF16, name="hb", bufs=4, align_bytes=64)
+            for u in range(QUART // HN):
+                j0 = QUART * q + HN * u
+                bank = psum.tile([P, PACK, HN], F32, name="h_bank", tag="h", bufs=3)
+                for a in range(PASSES):
+                    for t in range(PACK):
+                        nc.tensor.matmul_mx(
+                            out=bank[:, t, :],
+                            lhsT=w1_w[a, b][:, P * t : P * (t + 1)].bitcast(FP8X4),
+                            lhsT_scale=w1_s[a, b][:, P * t : P * (t + 1)],
+                            rhs=v_words(a, j0, HN),
+                            rhs_scale=v_s[4 * a : P, j0 : j0 + HN],
+                            start=(a == 0 and t == 0),
+                            stop=(a == PASSES - 1 and t == PACK - 1),
+                        )
+                nc.scalar.activation(out=hb[:, HN * u : HN * (u + 1), :], in_=bank[:].rearrange("p t j -> p j t"), func=ACT.Abs)
+            h_w[b, q] = keep.tile([P, QUART], U32, name="h_w%d%d" % (b, q), align_bytes=64)
+            h_s[b, q] = keep.tile([P, QUART], U8, name="h_s%d%d" % (b, q), align_bytes=64)
+            nc.vector.quantize_mx(out=h_w[b, q][:].bitcast(FP8X4), scales=h_s[b, q][:], in_=hb[:].rearrange("p j t -> p (j t)"))
+
+        def match_stage(q):
+            for mp in range(2):
+                bank = psum.tile([P, 2, QUART], F32, name="e_bank", tag="e", bufs=2)
+                for b in range(PASSES):
+                    for mi in range(2):
+                        m = 2 * mp + mi
+                        nc.tensor.matmul_mx(
+                            out=bank[:, mi, :],
+                            lhsT=v2_w[b][:, P * m : P * (m + 1)].bitcast(FP8X4),
+                            lhsT_scale=v2_s[4 * b : P, P * m : P * (m + 1)],
+                            rhs=h_w[b, q][:].bitcast(FP8X4),
+                            rhs_scale=h_s[b, q][:],
+                            start=(b == 0 and mi == 0),
+                            stop=(b == PASSES - 1 and mi == 1),
+                        )
+                bent = ring.tile([P, 2, QUART], F32, name="bent")
+                nc.vector.tensor_tensor(out=bent[:], in0=bank[:], in1=bend[q, mp][:], op=ALU.mult)
+                res = ring.tile([P, 2, QUART], F32, name="res", bufs=4)
+                for mi in range(2):
+                    m = 2 * mp + mi
+                    nc.vector.scalar_tensor_tensor(
+                        out=res[:, mi, :], in0=skip_bank[q, mp][:, mi, :], scalar=bias[:, m : m + 1], in1=bent[:, mi, :], op0=ALU.add, op1=ALU.add
+                    )
+                nc.sync.dma_start(
+                    out=out[2 * P * mp : 2 * P * (mp + 1), QUART * q : QUART * (q + 1)].rearrange("(mi p) j -> p mi j", p=P),
+                    in_=res[:],
+                )
+
+        gather_scales()
+        gather_scales2()
+        gather_v(0, 0, 4, "v00")
+        gather_v2(0, "v2_0")
+        g00 = grouped_tile(0, 0)
+        cast_w1("scalar", g00, raw00, 0, 0, P)
+        g10 = grouped_tile(1, 0)
+        cast_w1("vector", g10, raw10, 0, 0, 32)
+        cast_w1("scalar", g10, raw10, 0, 32, P)
+        quantize_w1(0, 0, g00, 1)
+        quantize_w1(1, 0, g10, 1)
+        gather_v(1, 0, 1, "v10")
+        gather_v(1, 1, 1, "v11")
+        gather_v(1, 2, 2, "v12")
+        g01 = grouped_tile(0, 1)
+        cast_w1("vector", g01, raw01, 0, 0, P)
+        quantize_w1(0, 1, g01, 1)
+        g11 = grouped_tile(1, 1)
+        cast_w1("vector", g11, raw11, 0, 0, 88)
+        h_stage(0, 0)
+        h_stage(0, 1)
+        skip_stage(0)
+        tanh_stage(0)
+        cast_w1("scalar", g11, raw11, 0, 88, P)
+        quantize_w1(1, 1, g11, 2)
+        gather_v2(1, "g11")
+        h_stage(0, 2)
+        h_stage(1, 0)
+        for q in range(NQ):
+            if q + 1 < NQ:
+                h_stage(1, q + 1)
+                skip_stage(q + 1)
+                tanh_stage(q + 1)
+            match_stage(q)
+            if q == 0:
+                h_stage(0, 3)

@@ -1,6 +1,7 @@
 from contextlib import ExitStack
 
 import concourse.mybir as mybir
+from concourse.masks import make_identity
 
 K, T, S, S2 = 1024, 2048, 1024, 512
 FLOPS = 2 * K * K * S + 2 * K * S2 * S + 2 * K * S2 * S
@@ -50,8 +51,8 @@ def tile_list_exam_clash_estimator_kernel(tc, tab_words, tab_scales, offs, offs2
             )
             return raw
 
-        def load_tab(a):
-            nc.sync.dma_start(out=tab_w[a][:], in_=tab_words[a].rearrange("p t i -> p (t i)").bitcast(I32))
+        def load_tab(a, t0, t1):
+            nc.sync.dma_start(out=tab_w[a][:, t0:t1], in_=tab_words[a].rearrange("p t i -> p (t i)").bitcast(I32)[:, t0:t1])
 
         def cast_w1(engine, grouped, raw, c0, m0, m1):
             dst = grouped[:, :, m0:m1, :].rearrange("p t m j -> p m j t")
@@ -99,31 +100,40 @@ def tile_list_exam_clash_estimator_kernel(tc, tab_words, tab_scales, offs, offs2
                 )
 
         def load_bias():
-            with nc.allow_non_contiguous_dma(reason="one bias value a partition"):
-                nc.sync.dma_start(out=bias[:], in_=b4.rearrange("(c p) -> p c", p=P))
+            nc.sync.dma_start(out=bias_rows[0 : S2 // P, :], in_=b4.rearrange("(c p) -> c p", p=P))
+            turned = psum.tile([P, P], F32, name="turned", tag="e", bufs=2)
+            nc.tensor.transpose(turned[:], bias_rows[:], ident[:])
+            nc.scalar.copy(out=bias[:], in_=turned[:, 0 : S2 // P])
 
         nc.gpsimd.memset(tab_s[:].bitcast(I32), 0)
+        bias_rows = keep.tile([P, P], F32, name="bias_rows")
+        ident = keep.tile([P, P], F32, name="ident")
+        nc.gpsimd.memset(bias_rows[:], 0.0)
+        make_identity(nc, ident[:])
         nc.gpsimd.memset(w4_s[:].bitcast(I32), 0)
         nc.gpsimd.memset(v_s1[:].bitcast(I32), 0)
         nc.sync.dma_start(idx[:], offs)
         nc.sync.dma_start(idx2[:], offs2)
-        load_w4_words()
+        load_tab(0, 0, 512)
         load_tab_scales()
-        load_tab(0)
-        raw00 = load_w1(0, 0, 0, KP, "raw00")
-        load_w4_scales()
+        load_tab(0, 512, T)
         load_bias()
+        raw00 = load_w1(0, 0, 0, KP, "raw00")
         raw10 = load_w1(1, 0, 0, KP, "raw10")
-        load_tab(1)
-        raw01 = load_w1(0, 1, 0, KP, "raw00")
-        raw11 = load_w1(1, 1, 0, KP, "raw10")
+        load_tab(1, 0, T)
+        raw01 = load_w1(0, 1, 0, KP, "raw01")
+        raw11 = load_w1(1, 1, 0, KP, "raw11")
+        load_w4_words()
+        load_w4_scales()
 
         v_s = keep.tile([P, S], U8, name="v_s", align_bytes=64)
         v2_s = keep.tile([P, S2], U8, name="v2_s", align_bytes=64)
 
         def gather_scales():
             nc.vector.tensor_copy(v_s[:], tab_s[:].indirect(idx[:]))
-            nc.gpsimd.dma_start(out=v_s1[0:100, :].bitcast(I32), in_=v_s[4:104, :].bitcast(I32))
+
+        def move_scales():
+            nc.sync.dma_start(out=v_s1[0:100, :].bitcast(I32), in_=v_s[4:104, :].bitcast(I32))
 
         def gather_scales2():
             nc.vector.tensor_copy(v2_s[:], tab_s[:].indirect(idx2[:]))
@@ -151,7 +161,7 @@ def tile_list_exam_clash_estimator_kernel(tc, tab_words, tab_scales, offs, offs2
         def skip_stage(q):
             j0 = QUART * q
             for mp in range(2):
-                bank = psum.tile([P, 2, QUART], F32, name="skip_bank", tag="skip", bufs=3)
+                bank = psum.tile([P, 2, QUART], F32, name="skip_bank", tag=("h" if q >= 3 else "skip"), bufs=3)
                 for a in range(PASSES):
                     for mi in range(2):
                         m = 2 * mp + mi
@@ -178,7 +188,7 @@ def tile_list_exam_clash_estimator_kernel(tc, tab_words, tab_scales, offs, offs2
         h_s = {}
 
         def h_stage(b, q):
-            hb = ring.tile([P, QUART, PACK], BF16, name="hb", bufs=4, align_bytes=64)
+            hb = ring.tile([P, QUART, PACK], BF16, name="hb", bufs=8, align_bytes=64)
             for u in range(QUART // HN):
                 j0 = QUART * q + HN * u
                 bank = psum.tile([P, PACK, HN], F32, name="h_bank", tag="h", bufs=3)
@@ -198,6 +208,8 @@ def tile_list_exam_clash_estimator_kernel(tc, tab_words, tab_scales, offs, offs2
             h_s[b, q] = keep.tile([P, QUART], U8, name="h_s%d%d" % (b, q), align_bytes=64)
             nc.vector.quantize_mx(out=h_w[b, q][:].bitcast(FP8X4), scales=h_s[b, q][:], in_=hb[:].rearrange("p j t -> p (j t)"))
 
+        e_bank = {}
+
         def match_stage(q):
             for mp in range(2):
                 bank = psum.tile([P, 2, QUART], F32, name="e_bank", tag="e", bufs=2)
@@ -213,8 +225,12 @@ def tile_list_exam_clash_estimator_kernel(tc, tab_words, tab_scales, offs, offs2
                             start=(b == 0 and mi == 0),
                             stop=(b == PASSES - 1 and mi == 1),
                         )
+                e_bank[q, mp] = bank
+
+        def finish_stage(q):
+            for mp in range(2):
                 bent = ring.tile([P, 2, QUART], F32, name="bent")
-                nc.vector.tensor_tensor(out=bent[:], in0=bank[:], in1=bend[q, mp][:], op=ALU.mult)
+                nc.vector.tensor_tensor(out=bent[:], in0=e_bank[q, mp][:], in1=bend[q, mp][:], op=ALU.mult)
                 res = ring.tile([P, 2, QUART], F32, name="res", bufs=4)
                 for mi in range(2):
                     m = 2 * mp + mi
@@ -227,15 +243,16 @@ def tile_list_exam_clash_estimator_kernel(tc, tab_words, tab_scales, offs, offs2
                 )
 
         gather_scales()
+        move_scales()
         gather_scales2()
         gather_v(0, 0, 4, "v00")
         gather_v2(0, "v2_0")
         g00 = grouped_tile(0, 0)
         cast_w1("scalar", g00, raw00, 0, 0, P)
+        quantize_w1(0, 0, g00, 1)
         g10 = grouped_tile(1, 0)
         cast_w1("vector", g10, raw10, 0, 0, 32)
         cast_w1("scalar", g10, raw10, 0, 32, P)
-        quantize_w1(0, 0, g00, 1)
         quantize_w1(1, 0, g10, 1)
         gather_v(1, 0, 1, "v10")
         gather_v(1, 1, 1, "v11")
@@ -244,21 +261,20 @@ def tile_list_exam_clash_estimator_kernel(tc, tab_words, tab_scales, offs, offs2
         cast_w1("vector", g01, raw01, 0, 0, P)
         quantize_w1(0, 1, g01, 1)
         g11 = grouped_tile(1, 1)
-        cast_w1("vector", g11, raw11, 0, 0, 88)
-        h_stage(0, 0)
-        h_stage(0, 1)
-        skip_stage(0)
-        tanh_stage(0)
-        cast_w1("scalar", g11, raw11, 0, 88, P)
+        cast_w1("vector", g11, raw11, 0, 0, P)
         quantize_w1(1, 1, g11, 2)
         gather_v2(1, "g11")
-        h_stage(0, 2)
-        h_stage(1, 0)
         for q in range(NQ):
+            h_stage(0, q)
+        h_stage(1, 0)
+        skip_stage(0)
+        tanh_stage(0)
+        h_stage(1, 1)
+        for q in range(NQ):
+            match_stage(q)
             if q + 1 < NQ:
-                h_stage(1, q + 1)
                 skip_stage(q + 1)
                 tanh_stage(q + 1)
-            match_stage(q)
-            if q == 0:
-                h_stage(0, 3)
+            if q + 2 < NQ:
+                h_stage(1, q + 2)
+            finish_stage(q)

@@ -32,12 +32,19 @@ def tile_list_exam_clash_estimator_kernel(tc, tab_words, tab_scales, offs, offs2
     with ExitStack() as ctx:
         keep = ctx.enter_context(tc.tile_pool(name="keep", bufs=1))
         ring = ctx.enter_context(tc.tile_pool(name="ring", bufs=3))
-        psum = ctx.enter_context(tc.psum_pool(name="psum", bufs=2))
+        psum = ctx.enter_context(tc.psum_pool(name="psum", bufs=1))
+
+        banks_taken = []
+
+        def next_bank(shape):
+            n = len(banks_taken)
+            banks_taken.append(psum.tile(shape, F32, name="bank%d" % n, tag="bank%d" % (n % 8)))
+            return banks_taken[n]
 
         idx = keep.tile([P, S // 16], U16, name="idx")
         idx2 = keep.tile([P, S2 // 16], U16, name="idx2")
         tab_s = keep.tile([P, T], U8, name="tab_s", tag="tab_s", align_bytes=64)
-        tab_w = [keep.tile([P, T], I32, name="tab_w%d" % a, align_bytes=64) for a in range(PASSES)]
+        tab_w = [keep.tile([P, T], I32, name="tab_w%d" % a, tag="tab_w%d" % a, align_bytes=64) for a in range(PASSES)]
         w4_w = keep.tile([P, PASSES, 2 * S2], U8, name="w4_w", align_bytes=64)
         w4_s = keep.tile([P, PASSES, S2], U8, name="w4_s", align_bytes=64)
         v_s1 = keep.tile([P, S], U8, name="v_s1", align_bytes=64)
@@ -55,8 +62,8 @@ def tile_list_exam_clash_estimator_kernel(tc, tab_words, tab_scales, offs, offs2
             nc.sync.dma_start(out=tab_w[a][:, t0:t1], in_=tab_words[a].rearrange("p t i -> p (t i)").bitcast(I32)[:, t0:t1])
 
         def cast_w1(engine, grouped, raw, c0, m0, m1):
-            dst = grouped[:, :, m0:m1, :].rearrange("p t m j -> p m j t")
-            src = raw[:, :, PACK * m0 - c0 : PACK * m1 - c0].rearrange("p j (m t) -> p m j t", t=PACK)
+            dst = grouped[:, :, m0:m1, :].rearrange("p t m j -> p m t j")
+            src = raw[:, :, PACK * m0 - c0 : PACK * m1 - c0].rearrange("p j (m t) -> p m t j", t=PACK)
             if engine == "scalar":
                 nc.scalar.copy(out=dst, in_=src)
             elif engine == "gpsimd":
@@ -101,7 +108,7 @@ def tile_list_exam_clash_estimator_kernel(tc, tab_words, tab_scales, offs, offs2
 
         def load_bias():
             nc.sync.dma_start(out=bias_rows[0 : S2 // P, :], in_=b4.rearrange("(c p) -> c p", p=P))
-            turned = psum.tile([P, P], F32, name="turned", tag="e", bufs=2)
+            turned = next_bank([P, P])
             nc.tensor.transpose(turned[:], bias_rows[:], ident[:])
             nc.scalar.copy(out=bias[:], in_=turned[:, 0 : S2 // P])
 
@@ -161,7 +168,7 @@ def tile_list_exam_clash_estimator_kernel(tc, tab_words, tab_scales, offs, offs2
         def skip_stage(q):
             j0 = QUART * q
             for mp in range(2):
-                bank = psum.tile([P, 2, QUART], F32, name="skip_bank", tag=("h" if q >= 3 else "skip"), bufs=3)
+                bank = next_bank([P, 2, QUART])
                 for a in range(PASSES):
                     for mi in range(2):
                         m = 2 * mp + mi
@@ -185,13 +192,16 @@ def tile_list_exam_clash_estimator_kernel(tc, tab_words, tab_scales, offs, offs2
                     nc.scalar.activation(out=bend[q, mp][:, mi, :], in_=skip_bank[q, mp][:, mi, :], func=ACT.Tanh, bias=bias[:, m : m + 1])
 
         h_w = {}
+        h_bf = {}
+        h_all = {}
+        h_tag = ["raw11", "h_w1"]
         h_s = {}
 
         def h_stage(b, q):
             hb = ring.tile([P, QUART, PACK], BF16, name="hb", bufs=8, align_bytes=64)
             for u in range(QUART // HN):
                 j0 = QUART * q + HN * u
-                bank = psum.tile([P, PACK, HN], F32, name="h_bank", tag="h", bufs=3)
+                bank = next_bank([P, PACK, HN])
                 for a in range(PASSES):
                     for t in range(PACK):
                         nc.tensor.matmul_mx(
@@ -204,15 +214,21 @@ def tile_list_exam_clash_estimator_kernel(tc, tab_words, tab_scales, offs, offs2
                             stop=(a == PASSES - 1 and t == PACK - 1),
                         )
                 nc.scalar.activation(out=hb[:, HN * u : HN * (u + 1), :], in_=bank[:].rearrange("p t j -> p j t"), func=ACT.Abs)
-            h_w[b, q] = keep.tile([P, QUART], U32, name="h_w%d%d" % (b, q), align_bytes=64)
+            h_bf[b, q] = hb
+
+        def quantize_h(b, q):
+            hb = h_bf[b, q]
+            if q == 0:
+                h_all[b] = keep.tile([P, S], U32, name="h_w%d" % b, tag=h_tag[b], align_bytes=64)
+            h_w[b, q] = h_all[b][:, QUART * q : QUART * (q + 1)]
             h_s[b, q] = keep.tile([P, QUART], U8, name="h_s%d%d" % (b, q), align_bytes=64)
-            nc.vector.quantize_mx(out=h_w[b, q][:].bitcast(FP8X4), scales=h_s[b, q][:], in_=hb[:].rearrange("p j t -> p (j t)"))
+            nc.vector.quantize_mx(out=h_w[b, q].bitcast(FP8X4), scales=h_s[b, q][:], in_=hb[:].rearrange("p j t -> p (j t)"))
 
         e_bank = {}
 
         def match_stage(q):
             for mp in range(2):
-                bank = psum.tile([P, 2, QUART], F32, name="e_bank", tag="e", bufs=2)
+                bank = next_bank([P, 2, QUART])
                 for b in range(PASSES):
                     for mi in range(2):
                         m = 2 * mp + mi
@@ -220,7 +236,7 @@ def tile_list_exam_clash_estimator_kernel(tc, tab_words, tab_scales, offs, offs2
                             out=bank[:, mi, :],
                             lhsT=v2_w[b][:, P * m : P * (m + 1)].bitcast(FP8X4),
                             lhsT_scale=v2_s[4 * b : P, P * m : P * (m + 1)],
-                            rhs=h_w[b, q][:].bitcast(FP8X4),
+                            rhs=h_w[b, q].bitcast(FP8X4),
                             rhs_scale=h_s[b, q][:],
                             start=(b == 0 and mi == 0),
                             stop=(b == PASSES - 1 and mi == 1),
@@ -237,10 +253,13 @@ def tile_list_exam_clash_estimator_kernel(tc, tab_words, tab_scales, offs, offs2
                     nc.vector.scalar_tensor_tensor(
                         out=res[:, mi, :], in0=skip_bank[q, mp][:, mi, :], scalar=bias[:, m : m + 1], in1=bent[:, mi, :], op0=ALU.add, op1=ALU.add
                     )
-                nc.sync.dma_start(
-                    out=out[2 * P * mp : 2 * P * (mp + 1), QUART * q : QUART * (q + 1)].rearrange("(mi p) j -> p mi j", p=P),
-                    in_=res[:],
-                )
+                    if q == NQ - 1:
+                        nc.sync.dma_start(out=out[P * m : P * (m + 1), QUART * q : QUART * (q + 1)], in_=res[:, mi, :])
+                if q < NQ - 1:
+                    nc.sync.dma_start(
+                        out=out[2 * P * mp : 2 * P * (mp + 1), QUART * q : QUART * (q + 1)].rearrange("(mi p) j -> p mi j", p=P),
+                        in_=res[:],
+                    )
 
         gather_scales()
         move_scales()
@@ -267,14 +286,19 @@ def tile_list_exam_clash_estimator_kernel(tc, tab_words, tab_scales, offs, offs2
         for q in range(NQ):
             h_stage(0, q)
         h_stage(1, 0)
+        quantize_h(0, 0)
+        quantize_h(1, 0)
         skip_stage(0)
         tanh_stage(0)
         h_stage(1, 1)
         for q in range(NQ):
             match_stage(q)
             if q + 1 < NQ:
-                skip_stage(q + 1)
-                tanh_stage(q + 1)
+                quantize_h(0, q + 1)
+                quantize_h(1, q + 1)
             if q + 2 < NQ:
                 h_stage(1, q + 2)
+            if q + 1 < NQ:
+                skip_stage(q + 1)
+                tanh_stage(q + 1)
             finish_stage(q)

@@ -34,12 +34,16 @@ def tile_list_exam_clash_estimator_kernel(tc, tab_words, tab_scales, offs, offs2
         ring = ctx.enter_context(tc.tile_pool(name="ring", bufs=3))
         psum = ctx.enter_context(tc.psum_pool(name="psum", bufs=1))
 
-        banks_taken = []
+        pair_of = {}
+        for q in range(NQ):
+            pair_of["h", 0, q] = q
+            pair_of["h", 1, q] = 1 if q == 1 else 0
+            pair_of["e", 0, q] = 3
+            pair_of["skip", 0, q] = 1 if q % 2 else 2
 
-        def next_bank(shape):
-            n = len(banks_taken)
-            banks_taken.append(psum.tile(shape, F32, name="bank%d" % n, tag="bank%d" % (n % 8)))
-            return banks_taken[n]
+        def bank_of(use, half, shape):
+            n = 2 * pair_of[use] + half
+            return psum.tile(shape, F32, name="bank_%s%d%d_%d" % (use + (half,)), tag="bank%d" % n)
 
         idx = keep.tile([P, S // 16], U16, name="idx")
         idx2 = keep.tile([P, S2 // 16], U16, name="idx2")
@@ -62,8 +66,8 @@ def tile_list_exam_clash_estimator_kernel(tc, tab_words, tab_scales, offs, offs2
             nc.sync.dma_start(out=tab_w[a][:, t0:t1], in_=tab_words[a].rearrange("p t i -> p (t i)").bitcast(I32)[:, t0:t1])
 
         def cast_w1(engine, grouped, raw, c0, m0, m1):
-            dst = grouped[:, :, m0:m1, :].rearrange("p t m j -> p m t j")
-            src = raw[:, :, PACK * m0 - c0 : PACK * m1 - c0].rearrange("p j (m t) -> p m t j", t=PACK)
+            dst = grouped[:, :, m0:m1, :].rearrange("p t m j -> p m j t")
+            src = raw[:, :, PACK * m0 - c0 : PACK * m1 - c0].rearrange("p j (m t) -> p m j t", t=PACK)
             if engine == "scalar":
                 nc.scalar.copy(out=dst, in_=src)
             elif engine == "gpsimd":
@@ -108,7 +112,7 @@ def tile_list_exam_clash_estimator_kernel(tc, tab_words, tab_scales, offs, offs2
 
         def load_bias():
             nc.sync.dma_start(out=bias_rows[0 : S2 // P, :], in_=b4.rearrange("(c p) -> c p", p=P))
-            turned = next_bank([P, P])
+            turned = psum.tile([P, P], F32, name="turned", tag="bank7")
             nc.tensor.transpose(turned[:], bias_rows[:], ident[:])
             nc.scalar.copy(out=bias[:], in_=turned[:, 0 : S2 // P])
 
@@ -168,7 +172,7 @@ def tile_list_exam_clash_estimator_kernel(tc, tab_words, tab_scales, offs, offs2
         def skip_stage(q):
             j0 = QUART * q
             for mp in range(2):
-                bank = next_bank([P, 2, QUART])
+                bank = bank_of(("skip", 0, q), mp, [P, 2, QUART])
                 for a in range(PASSES):
                     for mi in range(2):
                         m = 2 * mp + mi
@@ -194,14 +198,14 @@ def tile_list_exam_clash_estimator_kernel(tc, tab_words, tab_scales, offs, offs2
         h_w = {}
         h_bf = {}
         h_all = {}
-        h_tag = ["raw11", "h_w1"]
+        h_tag = {(0, 0): "raw11", (0, 2): "hb10", (1, 0): "h_w10", (1, 2): "h_w12"}
         h_s = {}
 
         def h_stage(b, q):
-            hb = ring.tile([P, QUART, PACK], BF16, name="hb", bufs=8, align_bytes=64)
+            hb = keep.tile([P, QUART, PACK], BF16, name="hb%d%d" % (b, q), tag="hb%d%d" % (b, q), align_bytes=64)
             for u in range(QUART // HN):
                 j0 = QUART * q + HN * u
-                bank = next_bank([P, PACK, HN])
+                bank = bank_of(("h", b, q), u, [P, PACK, HN])
                 for a in range(PASSES):
                     for t in range(PACK):
                         nc.tensor.matmul_mx(
@@ -218,9 +222,9 @@ def tile_list_exam_clash_estimator_kernel(tc, tab_words, tab_scales, offs, offs2
 
         def quantize_h(b, q):
             hb = h_bf[b, q]
-            if q == 0:
-                h_all[b] = keep.tile([P, S], U32, name="h_w%d" % b, tag=h_tag[b], align_bytes=64)
-            h_w[b, q] = h_all[b][:, QUART * q : QUART * (q + 1)]
+            if q % 2 == 0:
+                h_all[b] = keep.tile([P, HALF], U32, name="h_w%d%d" % (b, q), tag=h_tag[b, q], align_bytes=64)
+            h_w[b, q] = h_all[b][:, QUART * (q % 2) : QUART * (q % 2 + 1)]
             h_s[b, q] = keep.tile([P, QUART], U8, name="h_s%d%d" % (b, q), align_bytes=64)
             nc.vector.quantize_mx(out=h_w[b, q].bitcast(FP8X4), scales=h_s[b, q][:], in_=hb[:].rearrange("p j t -> p (j t)"))
 
@@ -228,7 +232,7 @@ def tile_list_exam_clash_estimator_kernel(tc, tab_words, tab_scales, offs, offs2
 
         def match_stage(q):
             for mp in range(2):
-                bank = next_bank([P, 2, QUART])
+                bank = bank_of(("e", 0, q), mp, [P, 2, QUART])
                 for b in range(PASSES):
                     for mi in range(2):
                         m = 2 * mp + mi

@@ -133,7 +133,8 @@ def tile_list_exam_clash_estimator_kernel(tc, tab_words, tab_scales, offs, offs2
         raw10 = load_w1(1, 0, 0, KP, "raw10")
         load_tab(1, 0, T)
         raw01 = load_w1(0, 1, 0, KP, "raw01")
-        raw11 = load_w1(1, 1, 0, KP, "raw11")
+        raw11a = load_w1(1, 1, 0, QUART, "raw11a")
+        raw11b = load_w1(1, 1, QUART, QUART, "raw11b")
         load_w4_words()
         load_w4_scales()
 
@@ -198,7 +199,7 @@ def tile_list_exam_clash_estimator_kernel(tc, tab_words, tab_scales, offs, offs2
         h_w = {}
         h_bf = {}
         h_all = {}
-        h_tag = {(0, 0): "raw11", (0, 2): "hb10", (1, 0): "h_w10", (1, 2): "h_w12"}
+        h_tag = {(0, 0): "raw11b", (0, 2): "hb10", (1, 0): "h_w10", (1, 2): "h_w12"}
         h_s = {}
 
         def h_stage(b, q):
@@ -274,8 +275,8 @@ def tile_list_exam_clash_estimator_kernel(tc, tab_words, tab_scales, offs, offs2
         cast_w1("scalar", g00, raw00, 0, 0, P)
         quantize_w1(0, 0, g00, 1)
         g10 = grouped_tile(1, 0)
-        cast_w1("vector", g10, raw10, 0, 0, 32)
-        cast_w1("scalar", g10, raw10, 0, 32, P)
+        cast_w1("vector", g10, raw10, 0, 0, 48)
+        cast_w1("scalar", g10, raw10, 0, 48, P)
         quantize_w1(1, 0, g10, 1)
         gather_v(1, 0, 1, "v10")
         gather_v(1, 1, 1, "v11")
@@ -284,7 +285,8 @@ def tile_list_exam_clash_estimator_kernel(tc, tab_words, tab_scales, offs, offs2
         cast_w1("vector", g01, raw01, 0, 0, P)
         quantize_w1(0, 1, g01, 1)
         g11 = grouped_tile(1, 1)
-        cast_w1("vector", g11, raw11, 0, 0, P)
+        cast_w1("vector", g11, raw11a, 0, 0, 64)
+        cast_w1("vector", g11, raw11b, QUART, 64, P)
         quantize_w1(1, 1, g11, 2)
         gather_v2(1, "g11")
         for q in range(NQ):

from contextlib import ExitStack

import concourse.mybir as mybir
from concourse.masks import make_identity

K, T, S, S2 = 1024, 2048, 1024, 512
FLOPS = 2 * K * K * S + 2 * K * S2 * S + 2 * K * S2 * S

F32 = mybir.dt.float32
BF16 = mybir.dt.bfloat16
I32 = mybir.dt.int32
U32 = mybir.dt.uint32
U16 = mybir.dt.uint16
U8 = mybir.dt.uint8
FP8X4 = mybir.dt.float8_e4m3fn_x4
FP4X4 = mybir.dt.float4_e2m1fn_x4
ACT = mybir.ActivationFunctionType
ALU = mybir.AluOpType

P = 128
PACK = 4
KP = P * PACK
PASSES = K // KP
HALF = 512
QUART = 256
NQ = S // QUART
HN = 128


def tile_list_exam_clash_estimator_kernel(tc, tab_words, tab_scales, offs, offs2, w1, w4_words, w4_scales, b4, out):
    nc = tc.nc
    with ExitStack() as ctx:
        keep = ctx.enter_context(tc.tile_pool(name="keep", bufs=1))
        ring = ctx.enter_context(tc.tile_pool(name="ring", bufs=3))
        psum = ctx.enter_context(tc.psum_pool(name="psum", bufs=1))

        pair_of = {}
        for q in range(NQ):
            pair_of["h", 0, q] = q
            pair_of["h", 1, q] = 1 if q == 1 else 0
            pair_of["e", 0, q] = 3
            pair_of["skip", 0, q] = 1 if q % 2 else 2

        def bank_of(use, half, shape):
            n = 2 * pair_of[use] + half
            return psum.tile(shape, F32, name="bank_%s%d%d_%d" % (use + (half,)), tag="bank%d" % n)

        idx = keep.tile([P, S // 16], U16, name="idx")
        idx2 = keep.tile([P, S2 // 16], U16, name="idx2")
        tab_s = keep.tile([P, T], U8, name="tab_s", tag="tab_s", align_bytes=64)
        tab_w = [keep.tile([P, T], I32, name="tab_w%d" % a, tag="tab_w%d" % a, align_bytes=64) for a in range(PASSES)]
        w4_w = keep.tile([P, PASSES, 2 * S2], U8, name="w4_w", align_bytes=64)
        w4_s = keep.tile([P, PASSES, S2], U8, name="w4_s", align_bytes=64)
        v_s1 = keep.tile([P, S], U8, name="v_s1", align_bytes=64)
        bias = keep.tile([P, S2 // P], F32, name="bias")

        def load_w1(a, b, c0, width, tag):
            raw = keep.tile([P, PACK, width], F32, name="raw%d%d_%d" % (a, b, c0), tag=tag, align_bytes=64)
            nc.sync.dma_start(
                out=raw[:],
                in_=w1[KP * a : KP * (a + 1), KP * b + c0 : KP * b + c0 + width].rearrange("(p j) c -> p j c", j=PACK),
            )
            return raw

        def load_tab(a, t0, t1):
            nc.sync.dma_start(out=tab_w[a][:, t0:t1], in_=tab_words[a].rearrange("p t i -> p (t i)").bitcast(I32)[:, t0:t1])

        def cast_w1(engine, grouped, raw, c0, m0, m1):
            dst = grouped[:, :, m0:m1, :].rearrange("p t m j -> p m j t")
            src = raw[:, :, PACK * m0 - c0 : PACK * m1 - c0].rearrange("p j (m t) -> p m j t", t=PACK)
            if engine == "scalar":
                nc.scalar.copy(out=dst, in_=src)
            elif engine == "gpsimd":
                nc.gpsimd.tensor_scalar(out=dst, in0=src, scalar1=1.0, scalar2=0.0, op0=ALU.mult, op1=ALU.add)
            else:
                nc.vector.tensor_copy(out=dst, in_=src)

        w1_w = {}
        w1_s = {}

        def quantize_w1(a, b, grouped, parts):
            w1_w[a, b] = keep.tile([P, KP], U32, name="w1_w%d%d" % (a, b), align_bytes=64)
            w1_s[a, b] = keep.tile([P, KP], U8, name="w1_s%d%d" % (a, b), align_bytes=64)
            nt = PACK // parts
            for part in range(parts):
                cols = slice(P * nt * part, P * nt * (part + 1))
                nc.vector.quantize_mx(
                    out=w1_w[a, b][:, cols].bitcast(FP8X4),
                    scales=w1_s[a, b][:, cols],
                    in_=grouped[:, nt * part : nt * (part + 1), :, :].rearrange("p t m j -> p (t m j)"),
                )

        def grouped_tile(a, b):
            return keep.tile([P, PACK, P, PACK], BF16, name="grouped%d%d" % (a, b), tag="g%d%d" % (a, b), align_bytes=64)

        def load_tab_scales():
            for quad in range(4):
                nc.sync.dma_start(
                    out=tab_s[32 * quad : 32 * quad + 8, :].bitcast(I32),
                    in_=tab_scales[:, 4 * quad : 4 * quad + 4, :].bitcast(I32),
                )

        def load_w4_words():
            nc.sync.dma_start(out=w4_w[:].bitcast(I32), in_=w4_words.rearrange("a p n -> p a n").bitcast(I32))

        def load_w4_scales():
            for quad in range(4):
                nc.sync.dma_start(
                    out=w4_s[32 * quad : 32 * quad + 4, :, :].bitcast(I32),
                    in_=w4_scales[:, 4 * quad : 4 * quad + 4, :].rearrange("a r n -> r a n").bitcast(I32),
                )

        def load_bias():
            nc.sync.dma_start(out=bias_rows[0 : S2 // P, :], in_=b4.rearrange("(c p) -> c p", p=P))
            turned = psum.tile([P, P], F32, name="turned", tag="bank7")
            nc.tensor.transpose(turned[:], bias_rows[:], ident[:])
            nc.scalar.copy(out=bias[:], in_=turned[:, 0 : S2 // P])

        nc.gpsimd.memset(tab_s[:].bitcast(I32), 0)
        bias_rows = keep.tile([P, P], F32, name="bias_rows")
        ident = keep.tile([P, P], F32, name="ident")
        nc.gpsimd.memset(bias_rows[:], 0.0)
        make_identity(nc, ident[:])
        nc.gpsimd.memset(w4_s[:].bitcast(I32), 0)
        nc.gpsimd.memset(v_s1[:].bitcast(I32), 0)
        nc.sync.dma_start(idx[:], offs)
        nc.sync.dma_start(idx2[:], offs2)
        load_tab(0, 0, 512)
        load_tab_scales()
        load_tab(0, 512, T)
        load_bias()
        raw00 = load_w1(0, 0, 0, KP, "raw00")
        raw10 = load_w1(1, 0, 0, KP, "raw10")
        load_tab(1, 0, T)
        raw01 = load_w1(0, 1, 0, KP, "raw01")
        raw11a = load_w1(1, 1, 0, QUART, "raw11a")
        raw11b = load_w1(1, 1, QUART, QUART, "raw11b")
        load_w4_words()
        load_w4_scales()

        v_s = keep.tile([P, S], U8, name="v_s", align_bytes=64)
        v2_s = keep.tile([P, S2], U8, name="v2_s", align_bytes=64)

        def gather_scales():
            nc.vector.tensor_copy(v_s[:], tab_s[:].indirect(idx[:]))

        def move_scales():
            nc.sync.dma_start(out=v_s1[0:100, :].bitcast(I32), in_=v_s[4:104, :].bitcast(I32))

        def gather_scales2():
            nc.vector.tensor_copy(v2_s[:], tab_s[:].indirect(idx2[:]))

        v_w = {}
        v2_w = {}

        def gather_v(a, q0, nq, tag):
            picked = keep.tile([P, nq * QUART], U32, name="v_w%d%d" % (a, q0), tag=tag, align_bytes=64)
            cols = slice(q0 * QUART // 16, (q0 + nq) * QUART // 16)
            nc.vector.tensor_copy(picked[:], tab_w[a][:].bitcast(U32).indirect(idx[:, cols]))
            for q in range(nq):
                v_w[a, q0 + q] = picked[:, QUART * q : QUART * (q + 1)]

        def gather_v2(a, tag):
            v2_w[a] = keep.tile([P, S2], U32, name="v2_w%d" % a, tag=tag, align_bytes=64)
            nc.vector.tensor_copy(v2_w[a][:], tab_w[a][:].bitcast(U32).indirect(idx2[:]))

        def v_words(a, j0, n):
            return v_w[a, j0 // QUART][:, j0 % QUART : j0 % QUART + n].bitcast(FP8X4)

        skip_bank = {}
        bend = {}

        def skip_stage(q):
            j0 = QUART * q
            for mp in range(2):
                bank = bank_of(("skip", 0, q), mp, [P, 2, QUART])
                for a in range(PASSES):
                    for mi in range(2):
                        m = 2 * mp + mi
                        plane = v_s if a == 0 else v_s1
                        nc.tensor.matmul_mx(
                            out=bank[:, mi, :],
                            lhsT=w4_w[:, a, 2 * P * m : 2 * P * (m + 1)].bitcast(FP4X4),
                            lhsT_scale=w4_s[:, a, P * m : P * (m + 1)],
                            rhs=v_words(a, j0, QUART),
                            rhs_scale=plane[:, j0 : j0 + QUART],
                            start=(a == 0 and mi == 0),
                            stop=(a == PASSES - 1 and mi == 1),
                        )
                skip_bank[q, mp] = bank

        def tanh_stage(q):
            for mp in range(2):
                bend[q, mp] = keep.tile([P, 2, QUART], F32, name="bend%d%d" % (q, mp))
                for mi in range(2):
                    m = 2 * mp + mi
                    nc.scalar.activation(out=bend[q, mp][:, mi, :], in_=skip_bank[q, mp][:, mi, :], func=ACT.Tanh, bias=bias[:, m : m + 1])

        h_w = {}
        h_bf = {}
        h_all = {}
        h_tag = {(0, 0): "raw11b", (0, 2): "hb10", (1, 0): "h_w10", (1, 2): "h_w12"}
        h_s = {}

        def h_stage(b, q):
            hb = keep.tile([P, QUART, PACK], BF16, name="hb%d%d" % (b, q), tag="hb%d%d" % (b, q), align_bytes=64)
            for u in range(QUART // HN):
                j0 = QUART * q + HN * u
                bank = bank_of(("h", b, q), u, [P, PACK, HN])
                for a in range(PASSES):
                    for t in range(PACK):
                        nc.tensor.matmul_mx(
                            out=bank[:, t, :],
                            lhsT=w1_w[a, b][:, P * t : P * (t + 1)].bitcast(FP8X4),
                            lhsT_scale=w1_s[a, b][:, P * t : P * (t + 1)],
                            rhs=v_words(a, j0, HN),
                            rhs_scale=v_s[4 * a : P, j0 : j0 + HN],
                            start=(a == 0 and t == 0),
                            stop=(a == PASSES - 1 and t == PACK - 1),
                        )
                nc.scalar.activation(out=hb[:, HN * u : HN * (u + 1), :], in_=bank[:].rearrange("p t j -> p j t"), func=ACT.Abs)
            h_bf[b, q] = hb

        def quantize_h(b, q):
            hb = h_bf[b, q]
            if q % 2 == 0:
                h_all[b] = keep.tile([P, HALF], U32, name="h_w%d%d" % (b, q), tag=h_tag[b, q], align_bytes=64)
            h_w[b, q] = h_all[b][:, QUART * (q % 2) : QUART * (q % 2 + 1)]
            h_s[b, q] = keep.tile([P, QUART], U8, name="h_s%d%d" % (b, q), align_bytes=64)
            nc.vector.quantize_mx(out=h_w[b, q].bitcast(FP8X4), scales=h_s[b, q][:], in_=hb[:].rearrange("p j t -> p (j t)"))

        e_bank = {}

        def match_stage(q):
            for mp in range(2):
                bank = bank_of(("e", 0, q), mp, [P, 2, QUART])
                for b in range(PASSES):
                    for mi in range(2):
                        m = 2 * mp + mi
                        nc.tensor.matmul_mx(
                            out=bank[:, mi, :],
                            lhsT=v2_w[b][:, P * m : P * (m + 1)].bitcast(FP8X4),
                            lhsT_scale=v2_s[4 * b : P, P * m : P * (m + 1)],
                            rhs=h_w[b, q].bitcast(FP8X4),
                            rhs_scale=h_s[b, q][:],
                            start=(b == 0 and mi == 0),
                            stop=(b == PASSES - 1 and mi == 1),
                        )
                e_bank[q, mp] = bank

        def finish_stage(q):
            for mp in range(2):
                bent = ring.tile([P, 2, QUART], F32, name="bent")
                nc.vector.tensor_tensor(out=bent[:], in0=e_bank[q, mp][:], in1=bend[q, mp][:], op=ALU.mult)
                res = ring.tile([P, 2, QUART], F32, name="res", bufs=4)
                for mi in range(2):
                    m = 2 * mp + mi
                    nc.vector.scalar_tensor_tensor(
                        out=res[:, mi, :], in0=skip_bank[q, mp][:, mi, :], scalar=bias[:, m : m + 1], in1=bent[:, mi, :], op0=ALU.add, op1=ALU.add
                    )
                    if q == NQ - 1:
                        nc.sync.dma_start(out=out[P * m : P * (m + 1), QUART * q : QUART * (q + 1)], in_=res[:, mi, :])
                if q < NQ - 1:
                    nc.sync.dma_start(
                        out=out[2 * P * mp : 2 * P * (mp + 1), QUART * q : QUART * (q + 1)].rearrange("(mi p) j -> p mi j", p=P),
                        in_=res[:],
                    )

        gather_scales()
        move_scales()
        gather_scales2()
        gather_v(0, 0, 4, "v00")
        gather_v2(0, "v2_0")
        g00 = grouped_tile(0, 0)
        cast_w1("scalar", g00, raw00, 0, 0, P)
        quantize_w1(0, 0, g00, 1)
        g10 = grouped_tile(1, 0)
        cast_w1("vector", g10, raw10, 0, 0, 48)
        cast_w1("scalar", g10, raw10, 0, 48, P)
        quantize_w1(1, 0, g10, 1)
        gather_v(1, 0, 1, "v10")
        gather_v(1, 1, 1, "v11")
        gather_v(1, 2, 2, "v12")
        g01 = grouped_tile(0, 1)
        cast_w1("vector", g01, raw01, 0, 0, P)
        quantize_w1(0, 1, g01, 1)
        g11 = grouped_tile(1, 1)
        cast_w1("vector", g11, raw11a, 0, 0, 64)
        cast_w1("vector", g11, raw11b, QUART, 64, P)
        quantize_w1(1, 1, g11, 2)
        gather_v2(1, "g11")
        for q in range(NQ):
            h_stage(0, q)
        h_stage(1, 0)
        quantize_h(0, 0)
        quantize_h(1, 0)
        skip_stage(0)
        tanh_stage(0)
        h_stage(1, 1)
        for q in range(NQ):
            match_stage(q)
            if q + 1 < NQ:
                quantize_h(0, q + 1)
                quantize_h(1, q + 1)
            if q + 2 < NQ:
                h_stage(1, q + 2)
            if q + 1 < NQ:
                skip_stage(q + 1)
                tanh_stage(q + 1)
            finish_stage(q)
